import numpy as np, ml_dtypes
CORES = [3,11,19,27,35,43]
N = 6
BF = ml_dtypes.bfloat16
def gentries(a):
    return np.ascontiguousarray(a.reshape(8, 16, -1).transpose(0, 2, 1)).reshape(8, -1)
def gtable(e):
    e = np.asarray(e); return np.ascontiguousarray(e.reshape(8, -1, 16).transpose(0, 2, 1)).reshape(128, -1).astype(np.int32)
def f(rng, *shape):
    return (rng.standard_normal(shape, dtype=np.float32) * np.exp2(rng.integers(-2, 3, shape[:-1] + (1,)))).astype(BF)
def wide(rng, *shape):
    v = f(rng, *shape).astype(np.float32); k = shape[:-2] + (1, shape[-1])
    return (v * np.exp2(rng.integers(-6, 7, k)) * (rng.random(k) > 0.0625)).astype(BF)
M, A, L, C, SR, SA = 3072, 512, 5, 3, 192, 64
def first(l):
    return M + N * SR + (l - 1) * (A + N * SA)
def glists(e):
    return np.stack([gtable(e[r].reshape(8, -1)) for r in range(N)])
def grow(rng, n):
    v = rng.standard_exponential((N, 8, 16, n), dtype=np.float32) * (rng.random((N, 8, 16, n)) < 0.75) * (0.5 + rng.random((N, 8, 1, n)))
    return np.add.accumulate(v, axis=2).reshape(N, 128, n).astype(BF)
def draw_parts(rng):
    e = np.zeros((N, 8, L, 2 * C, A), np.int64); k = (N, 8, 2 * C, A)
    for l in range(1, L + 1):
        e[:, :, l - 1] = rng.integers(0, first(l), k)
        if l > 1: e[:, :, l - 1] = np.where(rng.random(k) < 0.5, rng.integers(first(l - 1), first(l), k), e[:, :, l - 1])
    return e
def draw(rng, e):
    return {"sup": grow(rng, M), "cap": grow(rng, L * A), "stock": (8 * rng.random((N, 128, L * A)) * (rng.random((N, 128, L * A)) < 0.8)).astype(BF), "parts": glists(e),
            "ship": glists(rng.integers(0, M, (N, 8, N * SR))), "hand": glists(rng.integers(0, A, (N, 8, (L - 1) * N * SA)))}
def setup_inputs(rng):
    return draw(rng, draw_parts(rng))
def setup_inputs_ties(rng):
    e = draw_parts(rng); e[:, :, :, 1:C] = np.where(rng.random((N, 8, L, C - 1, A)) < 0.3, e[:, :, :, :1], e[:, :, :, 1:C])
    e[:, :, :, C:] = np.where(rng.random((N, 8, L, C, A)) < 0.2, e[:, :, :, :C], e[:, :, :, C:])
    d = draw(rng, e)
    d["sup"] = np.add.accumulate(rng.integers(0, 2, (N, 8, 16, M)), axis=2).reshape(N, 128, M).astype(np.float32).astype(BF)
    d["cap"] = np.add.accumulate(rng.integers(0, 3, (N, 8, 16, L * A)), axis=2).reshape(N, 128, L * A).astype(np.float32).astype(BF)
    d["stock"] = rng.integers(0, 4, (N, 128, L * A)).astype(np.float32).astype(BF); return d
def setup_inputs_ends(rng):
    e = draw_parts(rng)
    for l in range(1, L + 1):
        b = [0, M - 1, M, M + N * SR - 1]
        for m in range(1, l): b += [first(m), first(m) + A - 1, first(m) + A, first(m + 1) - 1]
        k = (N, 8, 2 * C, A); e[:, :, l - 1] = np.where(rng.random(k) < 0.5, rng.choice(np.array(b), k), e[:, :, l - 1])
        for r in range(N):
            q = (r + 1) % N
            for g in range(8):
                if l == 1: e[r, g, 0, 0, :SR] = M + q * SR + rng.permutation(SR)
                else: e[r, g, l - 1, 0, :SA] = first(l - 1) + A + q * SA + rng.permutation(SA)
    d = draw(rng, e)
    s = rng.integers(0, M, (N, 8, N, SR)); s[..., 0] = 0; s[..., -1] = M - 1; d["ship"] = glists(s)
    h = rng.integers(0, A, (N, 8, L - 1, N, SA)); h[..., 0] = A - 1; h[..., -1] = 0; d["hand"] = glists(h); return d
def setup_inputs_one(rng):
    e = np.zeros((N, 8, L, 2 * C, A), np.int64); a = rng.integers(1, N); k = (8, 2 * C, A)
    for r in range(N):
        q = (r + a) % N; e[r, :, 0] = M + q * SR + rng.integers(0, SR, k)
        for l in range(2, L + 1): e[r, :, l - 1] = first(l - 1) + A + q * SA + rng.integers(0, SA, k)
    d = draw(rng, e); s = rng.integers(0, M, (N, 8, N, SR)); q = rng.integers(0, N); s[q] = s[q][..., :1]; d["ship"] = glists(s); return d
def setup_inputs_late(rng):
    d = setup_inputs(rng); v = d["sup"].astype(np.float32).reshape(N, 8, 16, M); v[:, :, 15] = 64 - v[:, :, 14]; d["sup"] = v.reshape(N, 128, M).astype(BF)
    c = d["cap"].astype(np.float32).reshape(N, 8, 16, L * A); t = rng.integers(0, 14, (N, 8, 1, L * A))
    d["cap"] = np.where(np.arange(16)[:, None] < t - 4, np.float32(0), 8 * c).reshape(N, 128, L * A).astype(BF); return d
def setup_inputs_spread(rng):
    d = setup_inputs(rng)
    for k, n in (("sup", M), ("cap", L * A), ("stock", L * A)): d[k] = (wide(rng, N, 128, n).astype(np.float32) * np.float32(2.0 ** 40)).astype(BF)
    return d
def check_inputs(d):
    bad = []
    try:
        for k in ("sup", "cap", "stock"):
            v = d[k].astype(np.float32)
            if not (np.isfinite(v).all() and (np.abs(v) <= 2.0 ** 60).all()): bad.append(k)
        e = np.stack([gentries(v) for v in d["parts"]]).reshape(N, 8, L, 2 * C * A)
        if any((e[:, :, l - 1] < 0).any() or (e[:, :, l - 1] >= first(l)).any() for l in range(1, L + 1)): bad.append("parts")
        for k, n in (("ship", M), ("hand", A)):
            if (d[k] < 0).any() or (d[k] >= n).any(): bad.append(k)
    except Exception:
        bad.append("shapes")
    return bad
def reference(sup, cap, stock, parts, ship, hand):
    raw = sup.astype(np.float32).reshape(N, 8, 16, M); ca = cap.astype(np.float32).reshape(N, 8, 16, L, A); st = stock.astype(np.float32).reshape(N, 8, 16, L, A)
    e = [gentries(v).reshape(8, L, 1, 2 * C * A) for v in parts]; sh = [gentries(v).reshape(8, 1, N, SR) for v in ship]; ha = [gentries(v).reshape(8, 1, L - 1, N, SA) for v in hand]
    w = np.zeros((N, 8, 16, first(L)), np.float32); now = np.zeros((N, 8, 16, A), np.float32)
    w[..., :M] = raw; h = A // 2
    for r in range(N):
        for q in range(N): w[r, :, :, M + q * SR:M + (q + 1) * SR] = np.take_along_axis(raw[q], sh[q][:, :, r], 2)
    for l in range(1, L + 1):
        for r in range(N):
            v = np.take_along_axis(w[r], e[r][:, l - 1], 2).reshape(8, 16, 2 * C, A)
            i = np.argmin(v[:, 15, :C], axis=1)
            hit = np.arange(C)[:, None] == i[:, None]
            z = np.min(np.where(hit[:, None], v[:, :, C:], v[:, :, :C]), axis=2)
            s = np.zeros_like(z); s[:, 1:, :h] = z[:, :-1, :h]; s[:, 2:, h:] = z[:, :-2, h:]
            now[r] = np.minimum(s, ca[r, :, :, l - 1]) + st[r, :, :, l - 1]
        if l < L:
            b = first(l); w[:, :, :, b:b + A] = now
            for r in range(N):
                for q in range(N): w[r, :, :, b + A + q * SA:b + A + (q + 1) * SA] = np.take_along_axis(now[q], ha[q][:, :, l - 1, r], 2)
    return {"y": now.reshape(N, 128, A)}

from concourse.bass import DstId, RemoteDMATransfer
from concourse.mybir import AluOpType, ActivationFunctionType

N, M, A, L, SR, SA = 6, 3072, 512, 5, 192, 64
RAW = M + N * SR


def first(l):
    return RAW + (l - 1) * (A + N * SA)


CHUNKS = [(0, 128), (128, 256), (256, 384), (384, 512)]
ACHUNKS = [(0, 128), (128, 256), (256, 384), (384, 512)]
STAGE1 = [("S", "v0", 0, 1), ("V", "v2", 0, 1), ("S", "v0", 1, 2), ("V", "p2", 0, 1), ("S", "v0", 2, 3), ("V", "p2", 1, 2), ("V", "p1", 1, 2),
          ("S", "v2", 2, 3), ("S", "v0", 3, 4), ("V", "p2", 2, 3), ("S", "v2", 3, 4), ("V", "p2", 3, 4), ("S", "v2", 1, 2)]
THIRD = ["v2", "p1", "v2", "v2"]
FILL = [[("p1", 2, 4)], [("p1", 0, 1), ("p0", 2, 4)], [("p0", 0, 2)]]
OUTS = [(0, 2), (2, 4)]
RELAYED = 0

SCRATCH = {
    "W": ("sbuf", [128, first(L)], "float32"),
    "Wb": ("sbuf", [128, RAW], "bfloat16"),
    "capb": ("sbuf", [128, L * A], "bfloat16"),
    "stkb": ("sbuf", [128, L * A], "bfloat16"),
    "ck": ("sbuf", [128, A], "float32"),
    "PT": ("sbuf", [128, 960], "int32"),
    "shi": ("sbuf", [128, 72], "int32"),
    "hai": ("sbuf", [128, 96], "int32"),
    "shu": ("sbuf", [128, 72], "uint16"),
    "hau": ("sbuf", [128, 96], "uint16"),
    "sb0": ("sbuf", [128, N * SR], "bfloat16"),
    "sb1": ("sbuf", [128, (L - 1) * N * SA], "float32"),
    "ones": ("sbuf", [128, 384], "float32"),
    "mats": ("sbuf", [128, 384], "float32"),
    "matb": ("sbuf", [128, 384], "bfloat16"),
    "neg": ("sbuf", [128, 8], "float32"),
    "sel": ("sbuf", [128, 32], "float32"),
    "selb": ("sbuf", [128, 32], "bfloat16"),
    "pid": ("sbuf", [128, 1], "int32"),
    "odd": ("sbuf", [128, 1], "int32"),
    "mk": ("sbuf", [128, 2], "float32"),
    "X": ("sbuf", [128, 6, 32], "float32"),
    "XT": ("sbuf", [128, 6, 32], "float32"),
    "XS": ("sbuf", [128, 96], "float32"),
    "O1": ("sbuf", [128, 96], "uint16"),
    "O2": ("sbuf", [128, 64], "uint16"),
    "d1": ("sbuf", [128, 192], "float32"),
    "SC": ("sbuf", [128, 192], "float32"),
    "pos": ("sbuf", [128, 32], "int32"),
    "pos2": ("sbuf", [128, 32], "int32"),
    "Pf": ("sbuf", [128, 3 * A], "float32"),
    "Pb": ("sbuf", [128, 3 * A], "bfloat16"),
    "D": ("sbuf", [128, 272], "bfloat16"),
    "Y": ("sbuf", [128, A], "float32"),
    "E": ("psum", [128, 512], "float32"),
    "H": ("psum", [128, 512], "float32"),
    "CK": ("psum", [128, 512], "float32"),
    "U0": ("psum", [128, 512], "float32"),
    "U1": ("psum", [128, 512], "float32"),
    "U2": ("psum", [128, 512], "float32"),
    "U3": ("psum", [128, 512], "float32"),
}
for _n in ("v0", "v2", "al", "z"):
    SCRATCH[_n + "f"] = ("sbuf", [128, A], "float32")
    SCRATCH[_n + "b"] = ("sbuf", [128, A], "bfloat16")

SEMAPHORES = ["qV", "qS", "qP", "qG", "sent", "ldship", "ldsup", "ldhand", "out"] + ["arr%d" % i for i in range(L)] \
    + ["ldp%d" % i for i in range(1, L + 1)] + ["ldc%d" % i for i in range(1, L + 1)]


def emit(g, T, ops):
    Q = {"V": g.vector, "S": g.scalar, "P": g.tensor, "G": g, "Y": g.sync}
    deps, lastw, readers, bank = [], {}, {}, {}
    for i, (q, fn, rd, wr, bk, mark) in enumerate(ops):
        d = set()
        for k in rd:
            if k in lastw:
                d.add(lastw[k])
        for k in wr:
            if k in lastw and not (q == "P" and ops[lastw[k]][0] == "P"):
                d.add(lastw[k])
            d.update(readers.get(k, []))
        for k in bk:
            d.update(j for qq, j in bank.get(k, {}).items() if qq != q)
        d.discard(i)
        deps.append(d)
        for k in rd:
            readers.setdefault(k, []).append(i)
        for k in wr:
            lastw[k] = i
            readers[k] = []
        for k in bk:
            bank.setdefault(k, {})[q] = i
    needed = set()
    for d in deps:
        needed.update(d)
    count, done, know, total = {}, {}, {}, {}
    for i, (q, fn, rd, wr, bk, mark) in enumerate(ops):
        if mark is not None and mark[0] == "ext":
            done[i] = (mark[1], mark[2], {})
            total[mark[1]] = mark[2]
            continue
        kn = know.setdefault(q, {})
        for j in sorted(deps[i], reverse=True):
            s, c, ck = done[j]
            if s is None or kn.get(s, 0) >= c:
                continue
            Q[q].wait_ge(T.sem[s], c)
            kn[s] = c
            for s2, c2 in ck.items():
                kn[s2] = max(kn.get(s2, 0), c2)
        ins = fn()
        if mark is None:
            if i in needed:
                s = "q" + q
                count[s] = count.get(s, 0) + 1
                ins.then_inc(T.sem[s], 1)
                done[i] = (s, count[s], dict(kn))
                total[s] = count[s]
            else:
                done[i] = (None, 0, {})
        elif mark[0] == "remote":
            done[i] = (None, 0, {})
            total["sent"] = total.get("sent", 0) + mark[1]
        else:
            ins.then_inc(T.sem[mark[0]], mark[1])
            done[i] = (mark[0], mark[2], dict(kn))
            total[mark[0]] = mark[2]
    for s, c in total.items():
        g.wait_ge(T.sem[s], c)


def share(engines, n):
    per = 1
    while 2 * per * n <= len(engines):
        per *= 2
    return [engines[i * per:(i + 1) * per] for i in range(n)]


def routes(T, topo, rank):
    core = T.cores[rank]
    chip = topo.chip(core)
    others = [r for r in range(N) if r != rank]
    near = [r for r in others if topo.mates(chip, topo.chip(T.cores[r]))]
    plane = [r for r in others if topo.same_plane(chip, topo.chip(T.cores[r]))]
    twice = [r for r in others if r not in near and r not in plane]
    relayed = twice[:RELAYED]
    helpers = [c for c in topo.cores_of(core) if T.rank_of(c) is None and topo.die(c) != topo.die(core)
               and all(topo.may_write(c, T.cores[r]) for r in relayed)]
    direct = [r for r in sorted(twice + plane) + near if r not in relayed]
    off = topo.engines(core, T.cores[others[0]])
    together = 1
    while 2 * together <= len(direct):
        together *= 2
    calls = [[(r, T.cores[r], e) for r, e in zip(direct[:together], share(off, together))]]
    relay = {}
    if relayed:
        spare = [e for e in topo.engines(core, helpers[0]) if e not in off]
        for i, (r, e) in enumerate(zip(relayed, share(spare, len(relayed)))):
            calls[0].append((r, helpers[i], e))
            relay[helpers[i]] = [(r, T.cores[r], topo.engines(helpers[i], T.cores[r]))]
    rest = direct[together:]
    if rest:
        calls.append([(r, T.cores[r], e) for r, e in zip(rest, share(off, len(rest)))])
    return calls, relay


def piece(T, stage, r):
    if stage == 0:
        return T.sb0[:, r * SR:(r + 1) * SR]
    return T.sb1[:, ((stage - 1) * N + r) * SA:((stage - 1) * N + r + 1) * SA]


def slot(T, stage, q):
    if stage == 0:
        return T.Wb[:, M + q * SR:M + (q + 1) * SR]
    return T.W[:, first(stage) + A + q * SA:first(stage) + A + (q + 1) * SA]


def send(g, T, topo, call, stage, q):
    trs = []
    for r, c, eng in call:
        rid, pnc, _ = topo.addr(c)
        trs.append(RemoteDMATransfer(dst_ids=[DstId(rid=rid, pnc=pnc)], dma_engine_mask=sum(1 << e for e in eng),
                                     remote_sem=T.sem["arr%d" % stage], src=piece(T, stage, r),
                                     dst=slot(T, stage, q) if c == T.cores[r] else piece(T, stage, r)))
    return g.remote_dma_fused(trs, local_sem=T.sem.sent)


def landing(T, topo, core):
    n = 0
    for q in range(N):
        calls, relay = routes(T, topo, q)
        for call in calls + list(relay.values()):
            n += sum(len(e) for r, c, e in call if c == core)
    return n


def rank_program(g, core, T, topo):
    rank = T.rank_of(core)
    if rank is None:
        for q in range(N):
            call = routes(T, topo, q)[1].get(core)
            if call:
                for stage in range(L):
                    g.wait_ge(T.sem["arr%d" % stage], landing(T, topo, core))
                    send(g, T, topo, call, stage, q)
                g.wait_ge(T.sem.sent, L * sum(len(e) for r, c, e in call))
        return
    V, S, P, Y = g.vector, g.scalar, g.tensor, g.sync
    alu, COPY = AluOpType, ActivationFunctionType.Copy
    ops = []
    calls = routes(T, topo, rank)[0]

    def op(q, fn, rd=(), wr=(), bk=(), mark=None):
        ops.append([q, fn, list(rd), list(wr), list(bk), mark])

    def gather(q, out, win, off, rd, wr):
        if q == "S":
            op("S", lambda: S.activation(out, win.indirect(off), COPY), rd, wr)
        else:
            op("V", lambda: V.tensor_copy(out, win.indirect(off)), rd, wr)

    def hand_over(stage, win, offs, rd):
        w = SR if stage == 0 else SA
        sb, base = (T.sb0, 0) if stage == 0 else (T.sb1, (stage - 1) * N)
        head = sorted(r for r, c, e in calls[0])
        tail = [r for call in calls[1:] for r, c, e in call]
        half = (len(head) + 1) // 2
        for q, dst in (("V", head[:half]), ("S", head[half:]), ("V", tail)):
            runs = []
            for r in dst:
                if runs and runs[-1][-1] == r - 1:
                    runs[-1].append(r)
                else:
                    runs.append([r])
            for run in runs:
                a, b = run[0], run[-1] + 1
                gather(q, sb[:, (base + a) * w:(base + b) * w], win, offs(a * w // 16, b * w // 16), rd, ["sb%d.%d" % (stage, r) for r in run])
        gather("S", slot(T, stage, rank), win, offs(rank * w // 16, (rank + 1) * w // 16), rd, ["self%d" % stage])
        for call in calls:
            op("G", lambda call=call: send(g, T, topo, call, stage, rank), ["sb%d.%d" % (stage, r) for r, c, e in call], [], [],
               ("remote", sum(len(e) for r, c, e in call)))
        op("-", None, [], ["slots%d" % stage], [], ("ext", "arr%d" % stage, landing(T, topo, core)))

    def load(l, after):
        c = slice((l - 1) * A, l * A)
        pc = slice((l - 1) * 192, l * 192)
        op("Y", lambda: Y.dma_start(T.PT[:, pc], T.parts[:, pc]), after, ["PT%d" % l], [], ("ldp%d" % l, 16, 16))
        op("Y", lambda: Y.dma_start(T.capb[:, c], T.cap[:, c]), after, ["cap%d" % l], [], ("ldc%d" % l, 16, 32))
        op("Y", lambda: Y.dma_start(T.stkb[:, c], T.stock[:, c]), after, ["stk%d" % l], [], ("ldc%d" % l, 16, 32))

    def prepare(l):
        o = (l - 1) * 192
        pt = "PT%d" % l

        def col(i):
            return T.PT[:, o + 32 * i:o + 32 * i + 32]
        for h in range(2):
            op("V", lambda h=h: V.tensor_scalar(T.X[:, :, 16 * h:16 * h + 16], T.PT[:, o:o + 96], T.mk[:, h:h + 1], None, alu.mult),
               [pt, "mk"], ["X%d" % h])
        op("V", lambda: V.tensor_tensor(T.d1[:, 0:96:3], col(3), col(4), alu.subtract), [pt], ["d1a0"])
        op("V", lambda: V.transpose(T.XT[:], T.X[:]), ["X0", "X1"], ["XT"])
        op("V", lambda: V.tensor_tensor(T.d1[:, 1:96:3], col(4), col(5), alu.subtract), [pt], ["d1a1"])
        for h in range(2):
            op("V", lambda h=h: V.tensor_tensor(T.XS[:, h::2], T.XT[:, h::2, 0:16], T.XT[:, h::2, 16:32], alu.add), ["XT"], ["XS%d" % h])
        op("V", lambda: V.tensor_copy(T.d1[:, 2:96:3], col(5)), [pt], ["d1a2"])
        op("V", lambda: V.tensor_copy(T.O1[:], T.XS[:]), ["XS0", "XS1"], ["O1"])
        c = slice((l - 1) * A, l * A)
        op("P", lambda: P.matmul(T.CK[:], T.matb[:, 0:128], T.capb[:, c], True, False), ["matb", "cap%d" % l], ["CK"], ["CK"])
        op("P", lambda: P.matmul(T.CK[:], T.matb[:, 0:128], T.stkb[:, c], False, True), ["matb", "stk%d" % l], ["CK"], ["CK"])
        op("S", lambda: S.activation(T.ck[:], T.CK[:], COPY), ["CK"], ["ck"], ["CK"])
        for j, (a0, a1) in enumerate(CHUNKS):
            op("P", lambda j=j, a0=a0, a1=a1: P.matmul(T["U%d" % j][:, 0:a1 - a0], T.matb[:, 0:128],
                                                       T.stkb[:, (l - 1) * A + a0:(l - 1) * A + a1], True, False),
               ["stk%d" % l, "matb"], ["U%d" % j], ["U%d" % j])

    def level(l):
        x = "b" if l == 1 else "f"
        B = {n: T[n + x] for n in ("v0", "v2", "al", "z")}
        Pw = T["P" + x]

        def at(n, c0, c1):
            return Pw[:, A * int(n[1]) + c0:A * int(n[1]) + c1] if n[0] == "p" else B[n][:, c0:c1]
        sel, mats = (T.selb, T.matb) if l == 1 else (T.sel, T.mats)
        if l == 1:
            win, wk = T.Wb[:, 0:RAW], ["sup", "self0", "slots0"]
        else:
            win = T.W[:, 0:first(l)]
            wk = ["Wraw0", "Wraw1", "Wrs"]
            for m in range(1, l):
                wk += ["own%d.%d" % (m, j) for j in range(len(CHUNKS))] + ["self%d" % m, "slots%d" % m]
        if l < L:
            load(l + 1, ["slots%d" % (l - 1)])
        made = {"v0": (0, None), "v2": (2, None), "p0": (1, "v2"), "p1": (2, "v0"), "p2": (1, "v0")}

        def part(q, n, b0, b1):
            i, other = made[n]
            off = T.O1[:, 32 * i + 8 * b0:32 * i + 8 * b1]
            keys = ["%s%s.%d" % (n, x, b) for b in range(b0, b1)]
            if other is None:
                gather(q, at(n, 128 * b0, 128 * b1), win, off, wk + ["O1"], keys)
            else:
                op("V", lambda: V.tensor_tensor(at(n, 128 * b0, 128 * b1), win.indirect(off), at(other, 128 * b0, 128 * b1), alu.min),
                   wk + ["O1"] + ["%s%s.%d" % (other, x, b) for b in range(b0, b1)], keys)
        have, nxt = [], [0]
        for q, n, b0, b1 in STAGE1:
            part(q, n, b0, b1)
            have += [(n, b) for b in range(b0, b1)]
            while nxt[0] < 4 and all((m, nxt[0]) in have for m in ("v0", "p2", THIRD[nxt[0]])):
                b = nxt[0]
                three = sorted((("v0", 16), (THIRD[b], 0), ("p2", 8)), key=lambda e: have.index((e[0], b)))
                for i, (m, s0) in enumerate(three):
                    op("P", lambda b=b, m=m, s0=s0, i=i: P.matmul(T.E[:, b:64:4], at(m, 128 * b, 128 * b + 128), sel[:, s0:s0 + 16], i == 0, i == 2),
                       ["%s%s.%d" % (m, x, b), "sel"], ["E%d" % b], ["E"])
                nxt[0] += 1
        for e in FILL[0]:
            part("V", *e)
        op("V", lambda: V.tensor_scalar(T.D[:, 3:259:4], T.E[:, 0:64], 0.0, None, alu.is_ge), ["E%d" % b for b in range(4)], ["D"], ["E"])
        for v in range(2):
            for q in range(4):
                op("P", lambda v=v, q=q: P.matmul(T.H[:, 1 + v:96:3], T.D[:, 128 * v + 3 - q:128 * v + 131 - q],
                                                  T.matb[:, 32 * q:32 * q + 32], q == 0, q == 3), ["D", "matb"], ["H%d" % v], ["H"])
        for e in FILL[1]:
            part("V", *e)

        def scan(i, keys):
            c = slice(96 * i, 96 * i + 96)
            op("V", lambda: V.tensor_tensor_scan(T.SC[:, c], T.H[:, 0:96], T.d1[:, c], 0.0, alu.mult, alu.add),
               ["H0", "H1", "Hz"] + keys, ["SC%d" % i], ["H"])
        scan(0, ["d1a0", "d1a1", "d1a2"])
        scan(1, ["d1p"])
        op("V", lambda: V.tensor_copy(T.O2[:, 0:32], T.SC[:, 2:96:3]), ["SC0"], ["O2a"])
        op("V", lambda: V.tensor_copy(T.O2[:, 32:64], T.SC[:, 98:192:3]), ["SC1"], ["O2b"])
        for e in FILL[2]:
            part("V", *e)
        for a0, a1 in ACHUNKS:
            gather("S", B["al"][:, a0:a1], win, T.O2[:, a0 // 16:a1 // 16], wk + ["O2a"], ["al%s.%d" % (x, a0)])

        def z(j):
            a0, a1 = CHUNKS[j]
            op("V", lambda: V.tensor_tensor(B["z"][:, a0:a1], Pw[:].indirect(T.O2[:, 32 + a0 // 16:32 + a1 // 16]), B["al"][:, a0:a1], alu.min),
               ["O2b"] + ["p%d%s.%d" % (i, x, b) for i in range(3) for b in range(4)]
               + ["al%s.%d" % (x, u) for u, w in ACHUNKS if u < a1 and w > a0], ["z%s.%d" % (x, j)])
            U, u = T["U%d" % j], "U%d" % j
            s0 = 128 if a0 < A // 2 else 256
            op("P", lambda: P.matmul(U[:, 0:a1 - a0], mats[:, s0:s0 + 128], B["z"][:, a0:a1], False, True), ["z%s.%d" % (x, j), "matb"], [u], [u])

        def fin(j):
            a0, a1 = CHUNKS[j]
            U, u = T["U%d" % j], "U%d" % j
            out = T.W[:, first(l) + a0:first(l) + a1] if l < L else T.Y[:, a0:a1]
            op("V", lambda: V.tensor_tensor(out, U[:, 0:a1 - a0], T.ck[:, a0:a1], alu.min), [u, "ck"], ["own%d.%d" % (l, j)], [u])
            for i, (j0, j1) in enumerate(OUTS if l == L else []):
                if j == j1 - 1:
                    c = slice(CHUNKS[j0][0], a1)
                    op("YS"[i % 2], lambda i=i, c=c: (Y, S)[i % 2].dma_start(T.y[:, c], T.Y[:, c]),
                       ["own%d.%d" % (l, e) for e in range(j0, j1)], [], [], ("out", 16, 16 * len(OUTS)))
        n = len(CHUNKS)
        for j in range(n):
            z(j)
        for j in range(n):
            fin(j)
        if l < L:
            b = first(l)
            hand_over(l, T.W[:, b:b + A], lambda a, e: T.hau[:, (l - 1) * 24 + a:(l - 1) * 24 + e],
                      ["hau"] + ["own%d.%d" % (l, j) for j in range(n)])
            prepare(l + 1)
        if l == 1:
            op("S", lambda: S.activation(T.W[:, M:RAW], T.Wb[:, M:RAW], COPY), ["self0", "slots0"], ["Wrs"])

    op("Y", lambda: Y.dma_start(T.Wb[:, 0:M], T.sup[:]), [], ["sup"], [], ("ldsup", 16, 16))
    op("S", lambda: S.dma_start(T.shi[:], T.ship[:]), [], ["shi"], [], ("ldship", 16, 16))
    load(1, [])
    op("Y", lambda: Y.dma_start(T.hai[:], T.hand[:]), [], ["hai"], [], ("ldhand", 16, 16))
    op("V", lambda: V.memset(T.ones[:], 1.0), [], ["ones"])
    op("V", lambda: V.memset(T.neg[:], -1.0), [], ["neg"])
    op("V", lambda: V.memset(T.sel[:, 0:8], 0.0), [], ["sel0"])
    op("V", lambda: V.memset(T.sel[:, 24:32], 0.0), [], ["sel3"])
    op("V", lambda: V.memset(T.D[:], 0.0), [], ["D"])
    op("V", lambda: V.memset(T.d1[:, 96:192], -float(A)), [], ["d1z"])
    op("V", lambda: V.memset(T.H[:, 0:96], 0.0), [], ["Hz", "H0", "H1"], ["H"])
    op("G", lambda: g.iota(T.pid[:], [[0, 1]], 0, 1), [], ["pid"])
    op("G", lambda: g.iota(T.pos[:], [[1, 32]], 0, 32), [], ["pos"])
    op("G", lambda: g.affine_select(T.mats[:], T.ones[:], [[-1, 3], [1, 128]], alu.is_equal, 0.0, 0, -1), ["ones"], ["m0", "m1", "m2"])
    op("G", lambda: g.affine_select(T.sel[:, 8:16], T.ones[:, 0:8], [[-16, 8]], alu.is_equal, 0.0, -15, 1), ["ones"], ["sel1"])
    op("G", lambda: g.affine_select(T.sel[:, 16:24], T.neg[:], [[-16, 8]], alu.is_equal, 0.0, -15, 1), ["neg"], ["sel2"])
    op("V", lambda: V.tensor_scalar(T.odd[:], T.pid[:], 4, 1, alu.arith_shift_right, alu.bitwise_and), ["pid"], ["odd"])
    op("V", lambda: V.tensor_scalar(T.pos2[:], T.pos[:], A - 1, None, alu.bitwise_and), ["pos"], ["pos2"])
    op("V", lambda: V.tensor_copy(T.mk[:, 1:2], T.odd[:]), ["odd"], ["mk1"])
    op("V", lambda: V.tensor_scalar(T.d1[:, 98:192:3], T.pos2[:], float(2 * A), None, alu.add), ["pos2", "d1z"], ["d1p"])
    op("V", lambda: V.tensor_scalar(T.mk[:, 0:1], T.mk[:, 1:2], -1.0, 1.0, alu.mult, alu.add), ["mk1"], ["mk"])
    op("V", lambda: V.tensor_copy(T.shu[:], T.shi[:]), ["shi"], ["shu"])
    op("V", lambda: V.memset(T.mats[:, 128:384:16], 0.0), [], ["m1"])
    op("V", lambda: V.memset(T.mats[:, 257:384:16], 0.0), [], ["m2"])
    op("V", lambda: V.tensor_copy(T.selb[:], T.sel[:]), ["sel0", "sel1", "sel2", "sel3"], ["sel"])
    op("V", lambda: V.tensor_copy(T.matb[:], T.mats[:]), ["m0", "m1", "m2"], ["matb"])
    hand_over(0, T.Wb[:, 0:M], lambda a, e: T.shu[:, a:e], ["sup", "shu"])
    prepare(1)
    op("V", lambda: V.tensor_copy(T.hau[:], T.hai[:]), ["hai"], ["hau"])
    op("S", lambda: S.activation(T.W[:, 0:2048], T.Wb[:, 0:2048], COPY), ["sup"], ["Wraw0"])
    op("V", lambda: V.tensor_copy(T.W[:, 2048:M], T.Wb[:, 2048:M]), ["sup"], ["Wraw1"])
    for l in range(1, L + 1):
        level(l)
    emit(g, T, ops)
